import numpy as np
import ml_dtypes


def mxq(x, axis, fmt="e4m3"):
    dtype, down = {"e4m3": (ml_dtypes.float8_e4m3fn, 7), "e5m2": (ml_dtypes.float8_e5m2, 14)}[fmt]
    v = np.moveaxis(np.asarray(x, np.float32).astype(ml_dtypes.bfloat16).astype(np.float64), axis, -1)
    blocks = v.reshape(v.shape[:-1] + (-1, 32))
    amax = np.abs(blocks).max(-1, keepdims=True)
    byte = np.maximum(np.where(amax > 0, np.frexp(amax)[1] - 1 + 127, 0) - down, 1)
    scale = np.exp2(byte - 127.0)
    codes = (blocks / scale).astype(np.float32).astype(dtype).astype(np.float64)
    return np.moveaxis((codes * scale).reshape(v.shape), -1, axis)


WIDE = False


def mx_kscale(k):
    if not WIDE:
        return np.ones(k)
    levels = np.array([10, -10, 5, -5, 0])
    if k % 512:
        return np.exp2(np.random.permutation(np.resize(levels, k // 32))).repeat(32)
    a = np.empty((k // 512, 16))
    for p in range(k // 512):
        a[p, :8] = np.random.permutation(np.resize(levels, 8))
        for g in range(8):
            far = levels[np.abs(levels - a[p, g]) >= 10]
            a[p, g + 8] = far[np.random.randint(len(far))]
    return np.exp2(a.ravel()).repeat(32)


def f64(x):
    return np.asarray(x).astype(np.float64)


def striped(idx):
    return np.tile(idx.reshape(-1, 16).T, (8, 1)).astype(np.uint16)


def unstriped(offs):
    return offs[:16].T.reshape(-1).astype(np.int64)


def striped8(idx):
    return np.concatenate([x.reshape(-1, 16).T for x in idx]).astype(np.uint16)


def runs(offs, k):
    lists = np.stack([offs[16 * r : 16 * r + 16].T.reshape(-1) for r in range(8)]).astype(np.int64)
    return lists[np.arange(k) % 512 // 64]


def pack_weight(w):
    k, n = w.shape
    w = f64(np.asarray(w, np.float32).astype(ml_dtypes.bfloat16)).reshape(k // 32, 32, n)
    amax = np.abs(w).max(1)
    byte = np.clip(np.where(amax > 0, np.frexp(amax)[1] - 1 + 127 - 7, 1), 1, 254)
    scaled = (w * np.exp2(127.0 - byte)[:, None, :]).reshape(k, n).astype(np.float32)
    words = np.ascontiguousarray(scaled.reshape(k // 512, 128, 4, n).transpose(0, 1, 3, 2)).astype(ml_dtypes.float8_e4m3fn).view(np.uint8)
    return words, np.ascontiguousarray(byte.astype(np.uint8).reshape(k // 512, 16, n))


def unpack_weight(words, scales):
    g, p, n, _ = words.shape
    vals = np.ascontiguousarray(words).view(ml_dtypes.float8_e4m3fn).astype(np.float64) * np.repeat(np.exp2(scales.astype(np.float64) - 127.0), 8, axis=1)[..., None]
    return vals.transpose(0, 1, 3, 2).reshape(g * 512, n)


K, T, S, N, H = 512, 2048, 512, 512, 512


def setup_inputs():
    n = np.random.standard_normal
    s = mx_kscale(K)[:, None]
    u = mx_kscale(H)
    packed_xT = pack_weight(n((K, T)) * s)
    return {
        "x_words": packed_xT[0],
        "x_scales": packed_xT[1],
        "w1": (n((K, H)) / np.sqrt(K) / s).astype(np.float32),
        "gn": (np.random.uniform(0.5, 1.5, (H, 1)) * u[:, None]).astype(np.float32),
        "w2": (n((H, N)) / np.sqrt(H) / u[:, None]).astype(np.float32),
        "offs": striped(np.random.permutation(T)[:S]),
        "n1": striped8(np.stack([np.random.permutation(S) for _ in range(8)])),
        "n2": striped8(np.stack([np.random.permutation(S) for _ in range(8)])),
        "n3": striped8(np.stack([np.random.permutation(S) for _ in range(8)])),
        "n4": striped8(np.stack([np.random.permutation(S) for _ in range(8)])),
    }


def reference(x_words, x_scales, w1, gn, w2, offs, n1, n2, n3, n4):
    xq = unpack_weight(x_words, x_scales)[:, unstriped(offs)]
    y = mxq(f64(w1), 0, "e4m3").T @ xq
    pa = y[np.arange(H)[:, None], runs(n1, H)]
    pb = y[np.arange(H)[:, None], runs(n2, H)]
    z = f64(gn) * (np.maximum(np.maximum(y, pa), pb) - (0.5 * (np.minimum(np.minimum(y, pa), pb))))
    h = mxq(f64(w2), 0, "e4m3").T @ mxq(z, 0, "e4m3")
    return h - (np.minimum(h[np.arange(N)[:, None], runs(n3, N)], h[np.arange(N)[:, None], runs(n4, N)]))

@@ -1,0 +1,227 @@
+from contextlib import ExitStack
+
+import concourse.mybir as mybir
+
+K, T, S, H, N = 512, 2048, 512, 512, 512
+FLOPS = 2 * K * H * S + 2 * H * N * S
+
+F32 = mybir.dt.float32
+BF16 = mybir.dt.bfloat16
+I32 = mybir.dt.int32
+U32 = mybir.dt.uint32
+U16 = mybir.dt.uint16
+U8 = mybir.dt.uint8
+FP8X4 = mybir.dt.float8_e4m3fn_x4
+ALU = mybir.AluOpType
+ACT = mybir.ActivationFunctionType
+
+P = 128
+PACK = 4
+STRIPE = 16
+HALF = S // 2
+Z_CHUNKS = [(0, 256), (256, 384), (384, 512)]
+
+
+def tile_picked_layrangeunder_none_p_kernel(
+    tc, x_words, x_scales, w1, gn, w2, offs, n1, n2, n3, n4, out
+):
+    nc = tc.nc
+    with ExitStack() as ctx:
+        pool = ctx.enter_context(tc.tile_pool(name="sbuf", bufs=1))
+        psum = ctx.enter_context(tc.psum_pool(name="psum", bufs=1))
+
+        def sb(name, shape, dtype):
+            return pool.tile(shape, dtype, name=name, align_bytes=64)
+
+        def bank(b, width):
+            return psum.tile([P, width], F32, name="bank%d" % b)
+
+        def entries(lst, a, b):
+            return lst[:, a // STRIPE : b // STRIPE]
+
+        lists = {}
+
+        def load_list(name, src):
+            lists[name] = sb("list_" + name, [P, S // STRIPE], U16)
+            nc.sync.dma_start(lists[name][:], src)
+
+        xs_table = sb("xs_table", [P, T], U8)
+        nc.gpsimd.memset(xs_table[:].bitcast(I32), 0)
+        gain = sb("gain", [P, PACK], F32)
+        nc.scalar.dma_start(gain[:], gn.rearrange("(p t) o -> p (t o)", t=PACK))
+        load_list("offs", offs)
+        w1_rows = w1.rearrange("(p j) c -> p j c", j=PACK)
+        w1_raw = []
+        for u in range(2):
+            raw = sb("w1_raw%d" % u, [P, PACK, H // 2], F32)
+            nc.sync.dma_start(raw[:], w1_rows[:, :, u * (H // 2) : (u + 1) * (H // 2)])
+            w1_raw.append(raw)
+            if u == 0:
+                for q in range(4):
+                    nc.sync.dma_start(
+                        xs_table[32 * q : 32 * q + 4, :].bitcast(I32), x_scales[0, 4 * q : 4 * q + 4, :].bitcast(I32)
+                    )
+        xw_table = sb("xw_table", [P, T], U32)
+        nc.sync.dma_start(xw_table[:].bitcast(I32), x_words[0].rearrange("p n t -> p (n t)").bitcast(I32))
+        load_list("n1", n1)
+        load_list("n2", n2)
+        w2_raw = sb("w2_raw", [P, PACK, N], F32)
+        nc.sync.dma_start(w2_raw[:], w2.rearrange("(p j) c -> p j c", j=PACK))
+        load_list("n3", n3)
+        load_list("n4", n4)
+
+        half_gain = sb("half_gain", [P, PACK], F32)
+        gain_sign = sb("gain_sign", [P, PACK], F32)
+        nc.scalar.activation(half_gain[:], gain[:], ACT.Abs, scale=0.5)
+        nc.scalar.activation(gain_sign[:], gain[:], ACT.Sign)
+
+        xs = sb("xs", [P, S], U8)
+        nc.vector.tensor_copy(xs[:], xs_table[:].indirect(lists["offs"][:]))
+
+        w1_bf = sb("w1_bf", [P, PACK, P, PACK], BF16)
+        dealt = w1_bf[:].rearrange("p t m j -> p m j t")
+        nc.scalar.copy(dealt[:, : P // 2], w1_raw[0][:].rearrange("p j (m t) -> p m j t", t=PACK))
+        nc.vector.tensor_copy(dealt[:, P // 2 :], w1_raw[1][:].rearrange("p j (m t) -> p m j t", t=PACK))
+
+        def quantize_tile(name, src, t):
+            codes = sb("%s_codes%d" % (name, t), [P, P], U32)
+            scales = sb("%s_scales%d" % (name, t), [P, P], U8)
+            nc.vector.quantize_mx(codes[:].bitcast(FP8X4), scales[:], src[:, t].rearrange("p m j -> p (m j)"))
+            return codes, scales
+
+        def product(acc, weights, codes, scales):
+            nc.tensor.matmul_mx(
+                acc, lhsT=weights[0][:].bitcast(FP8X4), lhsT_scale=weights[1][:],
+                rhs=codes.bitcast(FP8X4), rhs_scale=scales, start=True, stop=True,
+            )
+
+        w1_q = [quantize_tile("w1", w1_bf, 0)]
+        xw = []
+        for u in range(2):
+            words = sb("xw%d" % u, [P, HALF], U32)
+            nc.vector.tensor_copy(words[:], xw_table[:].indirect(entries(lists["offs"], u * HALF, (u + 1) * HALF)))
+            xw.append(words)
+        for t in range(1, PACK):
+            w1_q.append(quantize_tile("w1", w1_bf, t))
+
+        y_win = [sb("y_win%d" % t, [P, S], F32) for t in range(PACK)]
+        y_own = [sb("y_own%d" % c, [P, PACK, b - a], F32) for c, (a, b) in enumerate(Z_CHUNKS)]
+        y_acc = {}
+        for t in range(PACK):
+            for u in range(2):
+                acc = bank(2 * t + u, HALF)
+                y_acc[t, u] = acc
+                product(acc[:], w1_q[t], xw[u][:], xs[:, u * HALF : (u + 1) * HALF])
+                nc.scalar.activation(
+                    y_win[t][:, u * HALF : (u + 1) * HALF], acc[:], ACT.Copy, scale=half_gain[:, t : t + 1]
+                )
+                if u == 0:
+                    nc.scalar.activation(y_own[0][:, t, :], acc[:], ACT.Copy, scale=half_gain[:, t : t + 1])
+        for c in range(1, len(Z_CHUNKS)):
+            a, b = Z_CHUNKS[c]
+            for t in range(PACK):
+                nc.scalar.activation(
+                    y_own[c][:, t, :], y_acc[t, 1][:, a - HALF : b - HALF], ACT.Copy, scale=half_gain[:, t : t + 1]
+                )
+
+        for j in range(PACK):
+            nc.scalar.activation(w2_raw[:, j, :], w2_raw[:, j, :], ACT.Copy, scale=gain_sign[:, j : j + 1])
+        w2_bf = sb("w2_bf", [P, PACK, P, PACK], BF16)
+        nc.scalar.copy(
+            w2_bf[:].rearrange("p t m j -> p m j t"), w2_raw[:].rearrange("p j (m t) -> p m j t", t=PACK)
+        )
+
+        da = [sb("da%d" % c, [P, PACK, b - a], F32) for c, (a, b) in enumerate(Z_CHUNKS)]
+        db = [sb("db%d" % c, [P, PACK, b - a], F32) for c, (a, b) in enumerate(Z_CHUNKS)]
+        hi = [sb("hi%d" % c, [P, PACK, b - a], F32) for c, (a, b) in enumerate(Z_CHUNKS)]
+        lo = [sb("lo%d" % c, [P, PACK, b - a], F32) for c, (a, b) in enumerate(Z_CHUNKS)]
+        z_bf = [sb("z_bf%d" % c, [P, b - a, PACK], BF16) for c, (a, b) in enumerate(Z_CHUNKS)]
+        z_codes = [sb("z_codes%d" % c, [P, b - a], U32) for c, (a, b) in enumerate(Z_CHUNKS)]
+        z_scales = [sb("z_scales%d" % c, [P, b - a], U8) for c, (a, b) in enumerate(Z_CHUNKS)]
+
+        def look_up_y(c, t):
+            a, b = Z_CHUNKS[c]
+            for dst, name in ((da, "n1"), (db, "n2")):
+                nc.vector.tensor_tensor(
+                    dst[c][:, t, :], y_win[t][:].indirect(entries(lists[name], a, b)), y_own[c][:, t, :], ALU.subtract
+                )
+
+        def extremes(c):
+            nc.vector.scalar_tensor_tensor(hi[c][:], da[c][:], 0.0, db[c][:], ALU.max, ALU.max)
+            nc.vector.scalar_tensor_tensor(lo[c][:], da[c][:], 0.0, db[c][:], ALU.min, ALU.min)
+
+        def spread(c):
+            nc.vector.scalar_tensor_tensor(hi[c][:], hi[c][:], 2.0, lo[c][:], ALU.mult, ALU.subtract)
+
+        def round_z(c):
+            nc.vector.tensor_tensor(
+                z_bf[c][:].rearrange("p (s i) t -> p s t i", i=2),
+                hi[c][:].rearrange("p t (s i) -> p s t i", i=2),
+                y_own[c][:].rearrange("p t (s i) -> p s t i", i=2),
+                ALU.add,
+            )
+
+        def quantize_z(c):
+            nc.vector.quantize_mx(z_codes[c][:].bitcast(FP8X4), z_scales[c][:], z_bf[c][:].rearrange("p s t -> p (s t)"))
+
+        h_win = [sb("h_win%d" % t, [P, S], F32) for t in range(PACK)]
+        h_own = [sb("h_own%d" % t, [P, S], F32) for t in range(PACK)]
+        w2_q = {}
+
+        def second_product(c, t):
+            a, b = Z_CHUNKS[c]
+            acc = bank(2 * t + c % 2, b - a)
+            product(acc[:], w2_q[t], z_codes[c][:], z_scales[c][:])
+            nc.scalar.activation(h_win[t][:, a:b], acc[:], ACT.Copy, scale=-1.0)
+            nc.scalar.activation(h_own[t][:, a:b], acc[:], ACT.Copy)
+
+        last = len(Z_CHUNKS) - 1
+        for t in range(PACK):
+            look_up_y(0, t)
+        extremes(0)
+        for c in range(1, last + 1):
+            look_up_y(c, 0)
+            spread(c - 1)
+            look_up_y(c, 1)
+            round_z(c - 1)
+            look_up_y(c, 2)
+            quantize_z(c - 1)
+            if c == 1:
+                w2_q[0] = quantize_tile("w2", w2_bf, 0)
+            second_product(c - 1, 0)
+            look_up_y(c, 3)
+            extremes(c)
+        spread(last)
+        w2_q[1] = quantize_tile("w2", w2_bf, 1)
+        round_z(last)
+        w2_q[2] = quantize_tile("w2", w2_bf, 2)
+        quantize_z(last)
+        second_product(last, 0)
+        w2_q[3] = quantize_tile("w2", w2_bf, 3)
+        for t in range(1, PACK):
+            for c in range(last + 1):
+                second_product(c, t)
+
+        out_rows = out.rearrange("(p t) s -> p t s", t=PACK)
+        pieces = [(t, a, a + HALF) for t in range(PACK - 1) for a in (0, HALF)]
+        pieces = pieces + [(PACK - 1, a, b) for a, b in Z_CHUNKS]
+        gaps = {}
+
+        def look_up_h(piece):
+            t, a, b = piece
+            for name in ("n3", "n4"):
+                gap = sb("gap_%s_%d_%d" % (name, t, a), [P, b - a], F32)
+                nc.vector.tensor_tensor(gap[:], h_win[t][:].indirect(entries(lists[name], a, b)), h_own[t][:, a:b], ALU.add)
+                gaps[name, piece] = gap
+
+        def finish(piece):
+            t, a, b = piece
+            res = sb("res_%d_%d" % (t, a), [P, b - a], F32)
+            nc.vector.tensor_tensor(res[:], gaps["n3", piece][:], gaps["n4", piece][:], ALU.max)
+            nc.sync.dma_start(out_rows[:, t, a:b], res[:])
+
+        look_up_h(pieces[0])
+        for before, piece in zip(pieces, pieces[1:]):
+            look_up_h(piece)
+            finish(before)
+        finish(pieces[-1])

@@ -1,6 +1,7 @@
 from contextlib import ExitStack
 
 import concourse.mybir as mybir
+from concourse.masks import make_identity
 
 K, T, S, H, N = 512, 2048, 512, 512, 512
 FLOPS = 2 * K * H * S + 2 * H * N * S
@@ -30,8 +31,8 @@ def tile_picked_layrangeunder_none_p_kernel(
         pool = ctx.enter_context(tc.tile_pool(name="sbuf", bufs=1))
         psum = ctx.enter_context(tc.psum_pool(name="psum", bufs=1))
 
-        def sb(name, shape, dtype):
-            return pool.tile(shape, dtype, name=name, align_bytes=64)
+        def sb(name, shape, dtype, tag=None):
+            return pool.tile(shape, dtype, name=name, tag=tag or name, align_bytes=64)
 
         def bank(b, width):
             return psum.tile([P, width], F32, name="bank%d" % b)
@@ -70,9 +71,14 @@ def tile_picked_layrangeunder_none_p_kernel(
         load_list("n3", n3)
         load_list("n4", n4)
 
+        ident = sb("ident", [P, P], F32)
+        make_identity(nc, ident[:])
+
         half_gain = sb("half_gain", [P, PACK], F32)
+        half_gain_neg = sb("half_gain_neg", [P, PACK], F32)
         gain_sign = sb("gain_sign", [P, PACK], F32)
         nc.scalar.activation(half_gain[:], gain[:], ACT.Abs, scale=0.5)
+        nc.scalar.activation(half_gain_neg[:], half_gain[:], ACT.Copy, scale=-1.0)
         nc.scalar.activation(gain_sign[:], gain[:], ACT.Sign)
 
         xs = sb("xs", [P, S], U8)
@@ -105,7 +111,8 @@ def tile_picked_layrangeunder_none_p_kernel(
             w1_q.append(quantize_tile("w1", w1_bf, t))
 
         y_win = [sb("y_win%d" % t, [P, S], F32) for t in range(PACK)]
-        y_own = [sb("y_own%d" % c, [P, PACK, b - a], F32) for c, (a, b) in enumerate(Z_CHUNKS)]
+        y_half = [sb("y_half%d" % u, [P, PACK, HALF], F32) for u in range(2)]
+        y_own = [y_half[a // HALF][:, :, a % HALF : a % HALF + b - a] for a, b in Z_CHUNKS]
         y_acc = {}
         for t in range(PACK):
             for u in range(2):
@@ -113,53 +120,101 @@ def tile_picked_layrangeunder_none_p_kernel(
                 y_acc[t, u] = acc
                 product(acc[:], w1_q[t], xw[u][:], xs[:, u * HALF : (u + 1) * HALF])
                 nc.scalar.activation(
-                    y_win[t][:, u * HALF : (u + 1) * HALF], acc[:], ACT.Copy, scale=half_gain[:, t : t + 1]
+                    y_win[t][:, u * HALF : (u + 1) * HALF], acc[:], ACT.Copy, scale=half_gain_neg[:, t : t + 1]
                 )
                 if u == 0:
-                    nc.scalar.activation(y_own[0][:, t, :], acc[:], ACT.Copy, scale=half_gain[:, t : t + 1])
-        for c in range(1, len(Z_CHUNKS)):
-            a, b = Z_CHUNKS[c]
-            for t in range(PACK):
-                nc.scalar.activation(
-                    y_own[c][:, t, :], y_acc[t, 1][:, a - HALF : b - HALF], ACT.Copy, scale=half_gain[:, t : t + 1]
-                )
+                    nc.scalar.activation(y_half[0][:, t, :], acc[:], ACT.Copy, scale=half_gain[:, t : t + 1])
+        for t in range(PACK):
+            nc.scalar.activation(y_half[1][:, t, :], y_acc[t, 1][:], ACT.Copy, scale=half_gain[:, t : t + 1])
 
         for j in range(PACK):
             nc.scalar.activation(w2_raw[:, j, :], w2_raw[:, j, :], ACT.Copy, scale=gain_sign[:, j : j + 1])
         w2_bf = sb("w2_bf", [P, PACK, P, PACK], BF16)
-        nc.scalar.copy(
-            w2_bf[:].rearrange("p t m j -> p m j t"), w2_raw[:].rearrange("p j (m t) -> p m j t", t=PACK)
-        )
 
-        da = [sb("da%d" % c, [P, PACK, b - a], F32) for c, (a, b) in enumerate(Z_CHUNKS)]
-        db = [sb("db%d" % c, [P, PACK, b - a], F32) for c, (a, b) in enumerate(Z_CHUNKS)]
-        hi = [sb("hi%d" % c, [P, PACK, b - a], F32) for c, (a, b) in enumerate(Z_CHUNKS)]
-        lo = [sb("lo%d" % c, [P, PACK, b - a], F32) for c, (a, b) in enumerate(Z_CHUNKS)]
-        z_bf = [sb("z_bf%d" % c, [P, b - a, PACK], BF16) for c, (a, b) in enumerate(Z_CHUNKS)]
+        def cast_w2(quarter):
+            rows = slice(quarter * P // 4, (quarter + 1) * P // 4)
+            nc.scalar.copy(
+                w2_bf[:].rearrange("p t m j -> p m j t")[:, rows],
+                w2_raw[:].rearrange("p j (m t) -> p m j t", t=PACK)[:, rows],
+            )
+
+        cast_w2(0)
+        cast_w2(1)
+
+        last = len(Z_CHUNKS) - 1
+        da, db, hi, lo, z_bf = {}, {}, {}, {}, {}
         z_codes = [sb("z_codes%d" % c, [P, b - a], U32) for c, (a, b) in enumerate(Z_CHUNKS)]
         z_scales = [sb("z_scales%d" % c, [P, b - a], U8) for c, (a, b) in enumerate(Z_CHUNKS)]
 
-        def look_up_y(c, t):
+        def look_up_y(c, t, tag=None):
             a, b = Z_CHUNKS[c]
+            if t == 0:
+                da[c] = sb("da%d" % c, [P, PACK, b - a], F32, tag)
+                db[c] = sb("db%d" % c, [P, PACK, b - a], F32)
             for dst, name in ((da, "n1"), (db, "n2")):
                 nc.vector.tensor_tensor(
-                    dst[c][:, t, :], y_win[t][:].indirect(entries(lists[name], a, b)), y_own[c][:, t, :], ALU.subtract
+                    dst[c][:, t, :], y_win[t][:].indirect(entries(lists[name], a, b)), y_own[c][:, t, :], ALU.add
                 )
 
         def extremes(c):
-            nc.vector.scalar_tensor_tensor(hi[c][:], da[c][:], 0.0, db[c][:], ALU.max, ALU.max)
-            nc.vector.scalar_tensor_tensor(lo[c][:], da[c][:], 0.0, db[c][:], ALU.min, ALU.min)
+            a, b = Z_CHUNKS[c]
+            lo[c] = sb("lo%d" % c, [P, PACK, b - a], F32)
+            hi[c] = sb("hi%d" % c, [P, PACK, b - a], F32)
+            for g in range((b - a) // P):
+                cols = slice(g * P, (g + 1) * P)
+                nc.vector.scalar_tensor_tensor(lo[c][:, :, cols], da[c][:, :, cols], 0.0, db[c][:, :, cols], ALU.min, ALU.min)
+                nc.vector.scalar_tensor_tensor(hi[c][:, :, cols], da[c][:, :, cols], 0.0, db[c][:, :, cols], ALU.max, ALU.max)
 
-        def spread(c):
-            nc.vector.scalar_tensor_tensor(hi[c][:], hi[c][:], 2.0, lo[c][:], ALU.mult, ALU.subtract)
+        def spread(c, tag):
+            a, b = Z_CHUNKS[c]
+            wide = sb("wide%d" % c, [P, PACK, b - a], F32, tag)
+            nc.vector.scalar_tensor_tensor(wide[:], lo[c][:], -2.0, hi[c][:], ALU.mult, ALU.add)
+            return wide
 
-        def round_z(c):
+        def round_z(c, wide):
+            a, b = Z_CHUNKS[c]
+            z_bf[c] = sb("z_bf%d" % c, [P, b - a, PACK], BF16)
             nc.vector.tensor_tensor(
                 z_bf[c][:].rearrange("p (s i) t -> p s t i", i=2),
-                hi[c][:].rearrange("p t (s i) -> p s t i", i=2),
-                y_own[c][:].rearrange("p t (s i) -> p s t i", i=2),
+                wide[:].rearrange("p t (s i) -> p s t i", i=2),
+                y_own[c].rearrange("p t (s i) -> p s t i", i=2),
                 ALU.add,
             )
+
+        def add_turned(sums, terms):
+            steps = [(i, g) for i in range(len(terms)) for g in range(len(terms[0]))]
+            for i, g in steps:
+                nc.tensor.matmul(
+                    sums[:, g * P : (g + 1) * P], terms[i][g], ident[:],
+                    start=(i, g) == steps[0], stop=(i, g) == steps[-1], is_transpose=True,
+                )
+
+        def sum_z_on_tensor(c):
+            a, b = Z_CHUNKS[c]
+            z_bf[c] = sb("z_bf%d" % c, [P, b - a, PACK], BF16)
+            for g in range((b - a) // P):
+                cols = slice(g * P, (g + 1) * P)
+                block = a // P + g
+                lo_twice = sb("lo_twice%d" % block, [P, PACK, P], F32, "chain%d" % min(block, 1))
+                nc.scalar.activation(lo_twice[:], lo[c][:, :, cols], ACT.Copy, scale=-2.0)
+                sums = bank(2 * (block % 2), PACK * P)
+                add_turned(
+                    sums,
+                    [
+                        [y_own[c][:, t, cols] for t in range(PACK)],
+                        [hi[c][:, t, cols] for t in range(PACK)],
+                        [lo_twice[:, t, :] for t in range(PACK)],
+                    ],
+                )
+                pairs = sb("pairs%d" % block, [P, 2, P, 2], BF16, "chain%d" % min(block, 1))
+                nc.scalar.copy(pairs[:], sums[:].rearrange("s (u e p) -> s u p e", u=2, e=2))
+                back = bank(4 + 2 * (block % 2), 2 * P)
+                pair_words = pairs[:].rearrange("s u p e -> s u (p e)").bitcast(F32)
+                for u in range(2):
+                    nc.tensor.transpose(back[:, u * P : (u + 1) * P], pair_words[:, u, :], ident[:])
+                nc.scalar.copy(
+                    z_bf[c][:, cols, :].bitcast(F32), back[:].rearrange("p (u s) -> p s u", u=2)
+                )
 
         def quantize_z(c):
             nc.vector.quantize_mx(z_codes[c][:].bitcast(FP8X4), z_scales[c][:], z_bf[c][:].rearrange("p s t -> p (s t)"))
@@ -170,41 +225,78 @@ def tile_picked_layrangeunder_none_p_kernel(
 
         def second_product(c, t):
             a, b = Z_CHUNKS[c]
-            acc = bank(2 * t + c % 2, b - a)
+            acc = bank(2 * t + 1, b - a)
             product(acc[:], w2_q[t], z_codes[c][:], z_scales[c][:])
             nc.scalar.activation(h_win[t][:, a:b], acc[:], ACT.Copy, scale=-1.0)
             nc.scalar.activation(h_own[t][:, a:b], acc[:], ACT.Copy)
 
-        last = len(Z_CHUNKS) - 1
-        for t in range(PACK):
-            look_up_y(0, t)
-        extremes(0)
-        for c in range(1, last + 1):
-            look_up_y(c, 0)
-            spread(c - 1)
-            look_up_y(c, 1)
-            round_z(c - 1)
-            look_up_y(c, 2)
-            quantize_z(c - 1)
-            if c == 1:
-                w2_q[0] = quantize_tile("w2", w2_bf, 0)
-            second_product(c - 1, 0)
-            look_up_y(c, 3)
+        for c in range(last):
+            for t in range(PACK):
+                look_up_y(c, t)
             extremes(c)
-        spread(last)
-        w2_q[1] = quantize_tile("w2", w2_bf, 1)
-        round_z(last)
-        w2_q[2] = quantize_tile("w2", w2_bf, 2)
+            sum_z_on_tensor(c)
+            if c == 0:
+                cast_w2(2)
+                cast_w2(3)
+        for t in range(PACK - 1):
+            w2_q[t] = quantize_tile("w2", w2_bf, t)
+        quantize_z(0)
+        for t in range(PACK - 1):
+            second_product(0, t)
+        for t in range(PACK):
+            look_up_y(last, t, "z_bf0")
+        extremes(last)
+        quantize_z(1)
+        second_product(1, 0)
+        wide = spread(last, "z_bf1")
+        w2_q[3] = quantize_tile("w2", w2_bf, 3)
+        round_z(last, wide)
         quantize_z(last)
         second_product(last, 0)
-        w2_q[3] = quantize_tile("w2", w2_bf, 3)
-        for t in range(1, PACK):
-            for c in range(last + 1):
-                second_product(c, t)
+        for t in range(1, PACK - 1):
+            second_product(1, t)
+            second_product(last, t)
 
         out_rows = out.rearrange("(p t) s -> p t s", t=PACK)
-        pieces = [(t, a, a + HALF) for t in range(PACK - 1) for a in (0, HALF)]
-        pieces = pieces + [(PACK - 1, a, b) for a, b in Z_CHUNKS]
+
+        def finish_on_tensor(t):
+            first = sb("first%d" % t, [P, S], F32)
+            rise = sb("rise%d" % t, [P, S], F32)
+            halves = [slice(u * HALF, (u + 1) * HALF) for u in range(2)]
+            for cols in halves:
+                nc.vector.tensor_copy(first[:, cols], h_win[t][:].indirect(entries(lists["n3"], cols.start, cols.stop)))
+            for u, cols in enumerate(halves):
+                nc.vector.tensor_tensor(
+                    rise[:, cols], h_win[t][:].indirect(entries(lists["n4"], cols.start, cols.stop)), first[:, cols], ALU.subtract
+                )
+                lift = sb("lift%d_%d" % (t, u), [P, HALF], F32, "half%d" % u)
+                nc.scalar.activation(lift[:], rise[:, cols], ACT.Relu)
+                sums = bank(2 * u, HALF)
+                blocks = [slice(g * P, (g + 1) * P) for g in range(HALF // P)]
+                add_turned(
+                    sums,
+                    [
+                        [h_own[t][:, cols][:, blk] for blk in blocks],
+                        [first[:, cols][:, blk] for blk in blocks],
+                        [lift[:, blk] for blk in blocks],
+                    ],
+                )
+                turned = sb("turned%d_%d" % (t, u), [P, HALF], F32, "half%d" % u)
+                nc.scalar.copy(turned[:], sums[:])
+                back = bank(4 + 2 * u, HALF)
+                for g in range(HALF // P):
+                    nc.tensor.transpose(back[:, g * P : (g + 1) * P], turned[:, g * P : (g + 1) * P], ident[:])
+                res = sb("res_%d_%d" % (t, u), [P, HALF], F32)
+                nc.scalar.copy(res[:], back[:])
+                nc.scalar.dma_start(out_rows[:, t, cols], res[:])
+
+        for t in range(PACK - 1):
+            finish_on_tensor(t)
+            if t == 0:
+                for c in range(last + 1):
+                    second_product(c, PACK - 1)
+
+        pieces = [(PACK - 1, a, b) for a, b in Z_CHUNKS]
         gaps = {}
 
         def look_up_h(piece):
@@ -216,7 +308,7 @@ def tile_picked_layrangeunder_none_p_kernel(
 
         def finish(piece):
             t, a, b = piece
-            res = sb("res_%d_%d" % (t, a), [P, b - a], F32)
+            res = sb("res_last_%d_%d" % (t, a), [P, b - a], F32)
             nc.vector.tensor_tensor(res[:], gaps["n3", piece][:], gaps["n4", piece][:], ALU.max)
             nc.sync.dma_start(out_rows[:, t, a:b], res[:])
 

@@ -48,8 +48,6 @@ def tile_picked_layrangeunder_none_p_kernel(
 
         xs_table = sb("xs_table", [P, T], U8)
         nc.gpsimd.memset(xs_table[:].bitcast(I32), 0)
-        gain = sb("gain", [P, PACK], F32)
-        nc.scalar.dma_start(gain[:], gn.rearrange("(p t) o -> p (t o)", t=PACK))
         load_list("offs", offs)
         w1_rows = w1.rearrange("(p j) c -> p j c", j=PACK)
         w1_raw = []
@@ -64,35 +62,39 @@ def tile_picked_layrangeunder_none_p_kernel(
                     )
         xw_table = sb("xw_table", [P, T], U32)
         nc.sync.dma_start(xw_table[:].bitcast(I32), x_words[0].rearrange("p n t -> p (n t)").bitcast(I32))
+        gain = sb("gain", [P, 8], F32)
+        for r in range(2):
+            nc.sync.dma_start(gain[r:P:2, 0:7], gn.rearrange("(a e) o -> a (e o)", e=8)[:, r : r + 7])
         load_list("n1", n1)
         load_list("n2", n2)
         w2_raw = sb("w2_raw", [P, PACK, N], F32)
-        nc.sync.dma_start(w2_raw[:], w2.rearrange("(p j) c -> p j c", j=PACK))
+        for r in range(2):
+            nc.sync.dma_start(w2_raw[r:P:2], w2.rearrange("(a j r) c -> r a j c", j=PACK, r=2)[r])
         load_list("n3", n3)
         load_list("n4", n4)
 
         ident = sb("ident", [P, P], F32)
         make_identity(nc, ident[:])
 
-        half_gain = sb("half_gain", [P, PACK], F32)
-        half_gain_neg = sb("half_gain_neg", [P, PACK], F32)
-        gain_sign = sb("gain_sign", [P, PACK], F32)
-        nc.scalar.activation(half_gain[:], gain[:], ACT.Abs, scale=0.5)
-        nc.scalar.activation(half_gain_neg[:], half_gain[:], ACT.Copy, scale=-1.0)
-        nc.scalar.activation(gain_sign[:], gain[:], ACT.Sign)
-
         xs = sb("xs", [P, S], U8)
         nc.vector.tensor_copy(xs[:], xs_table[:].indirect(lists["offs"][:]))
 
         w1_bf = sb("w1_bf", [P, PACK, P, PACK], BF16)
-        dealt = w1_bf[:].rearrange("p t m j -> p m j t")
-        nc.scalar.copy(dealt[:, : P // 2], w1_raw[0][:].rearrange("p j (m t) -> p m j t", t=PACK))
-        nc.vector.tensor_copy(dealt[:, P // 2 :], w1_raw[1][:].rearrange("p j (m t) -> p m j t", t=PACK))
+        dealt = w1_bf[:].rearrange("p t (a r) j -> p a t j r", r=2)
+        nc.scalar.copy(dealt[:, : P // 4], w1_raw[0][:].rearrange("p j (a t r) -> p a t j r", t=PACK, r=2))
+        nc.vector.tensor_copy(dealt[:, P // 4 :], w1_raw[1][:].rearrange("p j (a t r) -> p a t j r", t=PACK, r=2))
+
+        half_gain = sb("half_gain", [P, PACK], F32)
+        half_gain_neg = sb("half_gain_neg", [P, PACK], F32)
+        gain_sign = sb("gain_sign", [P, PACK], F32)
+        nc.scalar.activation(half_gain[:], gain[:, 0:7:2], ACT.Abs, scale=0.5)
+        nc.scalar.activation(half_gain_neg[:], half_gain[:], ACT.Copy, scale=-1.0)
+        nc.scalar.activation(gain_sign[:], gain[:, 0:7:2], ACT.Sign)
 
         def quantize_tile(name, src, t):
             codes = sb("%s_codes%d" % (name, t), [P, P], U32)
             scales = sb("%s_scales%d" % (name, t), [P, P], U8)
-            nc.vector.quantize_mx(codes[:].bitcast(FP8X4), scales[:], src[:, t].rearrange("p m j -> p (m j)"))
+            nc.vector.quantize_mx(codes[:].bitcast(FP8X4), scales[:], src.rearrange("p m j -> p (m j)"))
             return codes, scales
 
         def product(acc, weights, codes, scales):
@@ -101,60 +103,58 @@ def tile_picked_layrangeunder_none_p_kernel(
                 rhs=codes.bitcast(FP8X4), rhs_scale=scales, start=True, stop=True,
             )
 
-        w1_q = [quantize_tile("w1", w1_bf, 0)]
+        w1_q = [quantize_tile("w1", w1_bf[:, 0], 0)]
         xw = []
         for u in range(2):
             words = sb("xw%d" % u, [P, HALF], U32)
             nc.vector.tensor_copy(words[:], xw_table[:].indirect(entries(lists["offs"], u * HALF, (u + 1) * HALF)))
             xw.append(words)
         for t in range(1, PACK):
-            w1_q.append(quantize_tile("w1", w1_bf, t))
+            w1_q.append(quantize_tile("w1", w1_bf[:, t], t))
 
         y_win = [sb("y_win%d" % t, [P, S], F32) for t in range(PACK)]
         y_half = [sb("y_half%d" % u, [P, PACK, HALF], F32) for u in range(2)]
         y_own = [y_half[a // HALF][:, :, a % HALF : a % HALF + b - a] for a, b in Z_CHUNKS]
         y_acc = {}
+
+        def scaled_copy(dst, src, scale, on_vector):
+            if on_vector:
+                nc.vector.tensor_scalar(dst, src, scale, None, ALU.mult)
+            else:
+                nc.scalar.activation(dst, src, ACT.Copy, scale=scale)
+
         for t in range(PACK):
             for u in range(2):
                 acc = bank(2 * t + u, HALF)
                 y_acc[t, u] = acc
                 product(acc[:], w1_q[t], xw[u][:], xs[:, u * HALF : (u + 1) * HALF])
-                nc.scalar.activation(
-                    y_win[t][:, u * HALF : (u + 1) * HALF], acc[:], ACT.Copy, scale=half_gain_neg[:, t : t + 1]
-                )
+                scaled_copy(y_win[t][:, u * HALF : (u + 1) * HALF], acc[:], half_gain_neg[:, t : t + 1], (t, u) == (0, 0))
                 if u == 0:
-                    nc.scalar.activation(y_half[0][:, t, :], acc[:], ACT.Copy, scale=half_gain[:, t : t + 1])
+                    scaled_copy(y_half[0][:, t, :], acc[:], half_gain[:, t : t + 1], t == 0)
         for t in range(PACK):
             nc.scalar.activation(y_half[1][:, t, :], y_acc[t, 1][:], ACT.Copy, scale=half_gain[:, t : t + 1])
 
+        w2_signed = sb("w2_signed", [P, PACK, N], BF16)
         for j in range(PACK):
-            nc.scalar.activation(w2_raw[:, j, :], w2_raw[:, j, :], ACT.Copy, scale=gain_sign[:, j : j + 1])
-        w2_bf = sb("w2_bf", [P, PACK, P, PACK], BF16)
+            nc.scalar.activation(w2_signed[:, j, :], w2_raw[:, j, :], ACT.Copy, scale=gain_sign[:, j : j + 1])
+        w2_bf = [sb("w2_bf%d" % t, [P, P, PACK], BF16) for t in range(PACK)]
 
-        def cast_w2(quarter):
-            rows = slice(quarter * P // 4, (quarter + 1) * P // 4)
+        def deal_w2(t):
             nc.scalar.copy(
-                w2_bf[:].rearrange("p t m j -> p m j t")[:, rows],
-                w2_raw[:].rearrange("p j (m t) -> p m j t", t=PACK)[:, rows],
+                w2_bf[t][:].rearrange("p (a r) j -> p a j r", r=2),
+                w2_signed[:].rearrange("p j (a t r) -> p t a j r", t=PACK, r=2)[:, t],
             )
-
-        cast_w2(0)
-        cast_w2(1)
 
         last = len(Z_CHUNKS) - 1
         da, db, hi, lo, z_bf = {}, {}, {}, {}, {}
         z_codes = [sb("z_codes%d" % c, [P, b - a], U32) for c, (a, b) in enumerate(Z_CHUNKS)]
         z_scales = [sb("z_scales%d" % c, [P, b - a], U8) for c, (a, b) in enumerate(Z_CHUNKS)]
 
-        def look_up_y(c, t, tag=None):
+        def look_up_y(c, t, dst, name):
             a, b = Z_CHUNKS[c]
-            if t == 0:
-                da[c] = sb("da%d" % c, [P, PACK, b - a], F32, tag)
-                db[c] = sb("db%d" % c, [P, PACK, b - a], F32)
-            for dst, name in ((da, "n1"), (db, "n2")):
-                nc.vector.tensor_tensor(
-                    dst[c][:, t, :], y_win[t][:].indirect(entries(lists[name], a, b)), y_own[c][:, t, :], ALU.add
-                )
+            nc.vector.tensor_tensor(
+                dst[:, t, :], y_win[t][:].indirect(entries(lists[name], a, b)), y_own[c][:, t, :], ALU.add
+            )
 
         def extremes(c):
             a, b = Z_CHUNKS[c]
@@ -219,8 +219,11 @@ def tile_picked_layrangeunder_none_p_kernel(
         def quantize_z(c):
             nc.vector.quantize_mx(z_codes[c][:].bitcast(FP8X4), z_scales[c][:], z_bf[c][:].rearrange("p s t -> p (s t)"))
 
-        h_win = [sb("h_win%d" % t, [P, S], F32) for t in range(PACK)]
-        h_own = [sb("h_own%d" % t, [P, S], F32) for t in range(PACK)]
+        wide_tiles = range(1, PACK - 1)
+        h_win = [sb("h_win%d" % t, [P, 2 * S if t in wide_tiles else S], F32) for t in range(PACK)]
+        h_own = [
+            h_win[t + 1][:, S:] if t + 1 in wide_tiles else sb("h_own%d" % t, [P, S], F32)[:] for t in range(PACK)
+        ]
         w2_q = {}
 
         def second_product(c, t):
@@ -231,72 +234,45 @@ def tile_picked_layrangeunder_none_p_kernel(
             nc.scalar.activation(h_own[t][:, a:b], acc[:], ACT.Copy)
 
         for c in range(last):
+            a, b = Z_CHUNKS[c]
+            da[c] = sb("da%d" % c, [P, PACK, b - a], F32)
+            db[c] = sb("db%d" % c, [P, PACK, b - a], F32)
             for t in range(PACK):
-                look_up_y(c, t)
+                look_up_y(c, t, da[c], "n1")
+                look_up_y(c, t, db[c], "n2")
             extremes(c)
             sum_z_on_tensor(c)
-            if c == 0:
-                cast_w2(2)
-                cast_w2(3)
-        for t in range(PACK - 1):
-            w2_q[t] = quantize_tile("w2", w2_bf, t)
-        quantize_z(0)
-        for t in range(PACK - 1):
-            second_product(0, t)
+            deal_w2(2 * c)
+            deal_w2(2 * c + 1)
+        for t in range(2):
+            w2_q[t] = quantize_tile("w2", w2_bf[t][:], t)
+        da[last] = sb("da%d" % last, [P, PACK, P], F32)
         for t in range(PACK):
-            look_up_y(last, t, "z_bf0")
+            look_up_y(last, t, da[last], "n1")
+        quantize_z(0)
+        for t in range(2):
+            second_product(0, t)
+        db[last] = sb("db%d" % last, [P, PACK, P], F32, "z_bf0")
+        for t in range(PACK):
+            look_up_y(last, t, db[last], "n2")
         extremes(last)
         quantize_z(1)
         second_product(1, 0)
         wide = spread(last, "z_bf1")
-        w2_q[3] = quantize_tile("w2", w2_bf, 3)
+        w2_q[2] = quantize_tile("w2", w2_bf[2][:], 2)
         round_z(last, wide)
+        w2_q[3] = quantize_tile("w2", w2_bf[3][:], 3)
         quantize_z(last)
         second_product(last, 0)
-        for t in range(1, PACK - 1):
-            second_product(1, t)
-            second_product(last, t)
+        second_product(1, 1)
+        second_product(last, 1)
+        for t in range(2, PACK):
+            for c in range(last + 1):
+                second_product(c, t)
 
-        out_rows = out.rearrange("(p t) s -> p t s", t=PACK)
-
-        def finish_on_tensor(t):
-            first = sb("first%d" % t, [P, S], F32)
-            rise = sb("rise%d" % t, [P, S], F32)
-            halves = [slice(u * HALF, (u + 1) * HALF) for u in range(2)]
-            for cols in halves:
-                nc.vector.tensor_copy(first[:, cols], h_win[t][:].indirect(entries(lists["n3"], cols.start, cols.stop)))
-            for u, cols in enumerate(halves):
-                nc.vector.tensor_tensor(
-                    rise[:, cols], h_win[t][:].indirect(entries(lists["n4"], cols.start, cols.stop)), first[:, cols], ALU.subtract
-                )
-                lift = sb("lift%d_%d" % (t, u), [P, HALF], F32, "half%d" % u)
-                nc.scalar.activation(lift[:], rise[:, cols], ACT.Relu)
-                sums = bank(2 * u, HALF)
-                blocks = [slice(g * P, (g + 1) * P) for g in range(HALF // P)]
-                add_turned(
-                    sums,
-                    [
-                        [h_own[t][:, cols][:, blk] for blk in blocks],
-                        [first[:, cols][:, blk] for blk in blocks],
-                        [lift[:, blk] for blk in blocks],
-                    ],
-                )
-                turned = sb("turned%d_%d" % (t, u), [P, HALF], F32, "half%d" % u)
-                nc.scalar.copy(turned[:], sums[:])
-                back = bank(4 + 2 * u, HALF)
-                for g in range(HALF // P):
-                    nc.tensor.transpose(back[:, g * P : (g + 1) * P], turned[:, g * P : (g + 1) * P], ident[:])
-                res = sb("res_%d_%d" % (t, u), [P, HALF], F32)
-                nc.scalar.copy(res[:], back[:])
-                nc.scalar.dma_start(out_rows[:, t, cols], res[:])
-
-        for t in range(PACK - 1):
-            finish_on_tensor(t)
-            if t == 0:
-                for c in range(last + 1):
-                    second_product(c, PACK - 1)
-
-        pieces = [(PACK - 1, a, b) for a, b in Z_CHUNKS]
+        out_rows = out.rearrange("(a t r) s -> t a r s", t=PACK, r=2)
+        pieces = [(0, a, a + HALF) for a in (0, HALF)] + [(t, 0, S) for t in wide_tiles]
+        pieces = pieces + [(PACK - 1, a, b) for a, b in Z_CHUNKS]
         gaps = {}
 
         def look_up_h(piece):
@@ -310,7 +286,7 @@ def tile_picked_layrangeunder_none_p_kernel(
             t, a, b = piece
             res = sb("res_last_%d_%d" % (t, a), [P, b - a], F32)
             nc.vector.tensor_tensor(res[:], gaps["n3", piece][:], gaps["n4", piece][:], ALU.max)
-            nc.sync.dma_start(out_rows[:, t, a:b], res[:])
+            nc.sync.dma_start(out_rows[t, :, :, a:b], res[:])
 
         look_up_h(pieces[0])
         for before, piece in zip(pieces, pieces[1:]):

@@ -52,14 +52,12 @@ def tile_picked_layrangeunder_none_p_kernel(
         w1_rows = w1.rearrange("(p j) c -> p j c", j=PACK)
         w1_raw = []
         for u in range(2):
-            raw = sb("w1_raw%d" % u, [P, PACK, H // 2], F32)
-            nc.sync.dma_start(raw[:], w1_rows[:, :, u * (H // 2) : (u + 1) * (H // 2)])
+            raw = sb("w1_raw%d" % u, [P, 2, H], F32)
+            nc.sync.dma_start(raw[:], w1_rows[:, 2 * u : 2 * u + 2, :])
             w1_raw.append(raw)
             if u == 0:
-                for q in range(4):
-                    nc.sync.dma_start(
-                        xs_table[32 * q : 32 * q + 4, :].bitcast(I32), x_scales[0, 4 * q : 4 * q + 4, :].bitcast(I32)
-                    )
+                for r in range(4):
+                    nc.sync.dma_start(xs_table[r:P:32, :].bitcast(I32), x_scales[0, r:16:4, :].bitcast(I32))
         xw_table = sb("xw_table", [P, T], U32)
         nc.sync.dma_start(xw_table[:].bitcast(I32), x_words[0].rearrange("p n t -> p (n t)").bitcast(I32))
         gain = sb("gain", [P, 8], F32)
@@ -81,8 +79,8 @@ def tile_picked_layrangeunder_none_p_kernel(
 
         w1_bf = sb("w1_bf", [P, PACK, P, PACK], BF16)
         dealt = w1_bf[:].rearrange("p t (a r) j -> p a t j r", r=2)
-        nc.scalar.copy(dealt[:, : P // 4], w1_raw[0][:].rearrange("p j (a t r) -> p a t j r", t=PACK, r=2))
-        nc.vector.tensor_copy(dealt[:, P // 4 :], w1_raw[1][:].rearrange("p j (a t r) -> p a t j r", t=PACK, r=2))
+        nc.scalar.copy(dealt[:, :, :, 0:2], w1_raw[0][:].rearrange("p j (a t r) -> p a t j r", t=PACK, r=2))
+        nc.vector.tensor_copy(dealt[:, :, :, 2:4], w1_raw[1][:].rearrange("p j (a t r) -> p a t j r", t=PACK, r=2))
 
         half_gain = sb("half_gain", [P, PACK], F32)
         half_gain_neg = sb("half_gain_neg", [P, PACK], F32)
@@ -219,7 +217,7 @@ def tile_picked_layrangeunder_none_p_kernel(
         def quantize_z(c):
             nc.vector.quantize_mx(z_codes[c][:].bitcast(FP8X4), z_scales[c][:], z_bf[c][:].rearrange("p s t -> p (s t)"))
 
-        wide_tiles = range(1, PACK - 1)
+        wide_tiles = range(2, PACK - 1)
         h_win = [sb("h_win%d" % t, [P, 2 * S if t in wide_tiles else S], F32) for t in range(PACK)]
         h_own = [
             h_win[t + 1][:, S:] if t + 1 in wide_tiles else sb("h_own%d" % t, [P, S], F32)[:] for t in range(PACK)
@@ -261,8 +259,8 @@ def tile_picked_layrangeunder_none_p_kernel(
         wide = spread(last, "z_bf1")
         w2_q[2] = quantize_tile("w2", w2_bf[2][:], 2)
         round_z(last, wide)
-        w2_q[3] = quantize_tile("w2", w2_bf[3][:], 3)
         quantize_z(last)
+        w2_q[3] = quantize_tile("w2", w2_bf[3][:], 3)
         second_product(last, 0)
         second_product(1, 1)
         second_product(last, 1)
@@ -271,7 +269,42 @@ def tile_picked_layrangeunder_none_p_kernel(
                 second_product(c, t)
 
         out_rows = out.rearrange("(a t r) s -> t a r s", t=PACK, r=2)
-        pieces = [(0, a, a + HALF) for a in (0, HALF)] + [(t, 0, S) for t in wide_tiles]
+
+        def finish_on_tensor(t):
+            first = sb("first%d" % t, [P, S], F32)
+            rise = sb("rise%d" % t, [P, S], F32)
+            halves = [slice(u * HALF, (u + 1) * HALF) for u in range(2)]
+            for cols in halves:
+                nc.vector.tensor_copy(first[:, cols], h_win[t][:].indirect(entries(lists["n3"], cols.start, cols.stop)))
+            for u, cols in enumerate(halves):
+                nc.vector.tensor_tensor(
+                    rise[:, cols], h_win[t][:].indirect(entries(lists["n4"], cols.start, cols.stop)), first[:, cols], ALU.subtract
+                )
+                lift = sb("lift%d_%d" % (t, u), [P, HALF], F32, "half%d" % u)
+                nc.scalar.activation(lift[:], rise[:, cols], ACT.Relu)
+                sums = bank(2 * u, HALF)
+                blocks = [slice(g * P, (g + 1) * P) for g in range(HALF // P)]
+                add_turned(
+                    sums,
+                    [
+                        [h_own[t][:, cols][:, blk] for blk in blocks],
+                        [first[:, cols][:, blk] for blk in blocks],
+                        [lift[:, blk] for blk in blocks],
+                    ],
+                )
+                turned = sb("turned%d_%d" % (t, u), [P, HALF], F32, "half%d" % u)
+                nc.scalar.copy(turned[:], sums[:])
+                back = bank(4 + 2 * u, HALF)
+                for g in range(HALF // P):
+                    nc.tensor.transpose(back[:, g * P : (g + 1) * P], turned[:, g * P : (g + 1) * P], ident[:])
+                res = sb("res_%d_%d" % (t, u), [P, HALF], F32)
+                nc.scalar.copy(res[:], back[:])
+                nc.sync.dma_start(out_rows[t, :, :, cols], res[:])
+
+        for t in range(2):
+            finish_on_tensor(t)
+
+        pieces = [(t, 0, S) for t in wide_tiles]
         pieces = pieces + [(PACK - 1, a, b) for a, b in Z_CHUNKS]
         gaps = {}
 

@@ -20,7 +20,10 @@ P = 128
 PACK = 4
 STRIPE = 16
 HALF = S // 2
-Z_CHUNKS = [(0, 256), (256, 384), (384, 512)]
+RANGES = [(0, 256), (256, 384), (384, 512)]
+LAST = len(RANGES) - 1
+TURNED_PLANES = 2
+WIDE_PLANE = 2
 
 
 def tile_picked_layrangeunder_none_p_kernel(
@@ -34,11 +37,8 @@ def tile_picked_layrangeunder_none_p_kernel(
         def sb(name, shape, dtype, tag=None):
             return pool.tile(shape, dtype, name=name, tag=tag or name, align_bytes=64)
 
-        def bank(b, width):
-            return psum.tile([P, width], F32, name="bank%d" % b)
-
-        def entries(lst, a, b):
-            return lst[:, a // STRIPE : b // STRIPE]
+        def bank(number, width):
+            return psum.tile([P, width], F32, name="bank%d" % number)
 
         lists = {}
 
@@ -46,23 +46,27 @@ def tile_picked_layrangeunder_none_p_kernel(
             lists[name] = sb("list_" + name, [P, S // STRIPE], U16)
             nc.sync.dma_start(lists[name][:], src)
 
+        def entries(name, a, b):
+            return lists[name][:, a // STRIPE : b // STRIPE]
+
         xs_table = sb("xs_table", [P, T], U8)
         nc.gpsimd.memset(xs_table[:].bitcast(I32), 0)
         load_list("offs", offs)
         w1_rows = w1.rearrange("(p j) c -> p j c", j=PACK)
         w1_raw = []
-        for u in range(2):
-            raw = sb("w1_raw%d" % u, [P, 2, H], F32)
-            nc.sync.dma_start(raw[:], w1_rows[:, 2 * u : 2 * u + 2, :])
+        for pair in range(2):
+            raw = sb("w1_raw%d" % pair, [P, 2, H], F32)
+            nc.sync.dma_start(raw[:], w1_rows[:, 2 * pair : 2 * pair + 2, :])
             w1_raw.append(raw)
-            if u == 0:
-                for r in range(4):
-                    nc.sync.dma_start(xs_table[r:P:32, :].bitcast(I32), x_scales[0, r:16:4, :].bitcast(I32))
+            if pair == 0:
+                for e in range(4):
+                    nc.sync.dma_start(xs_table[e:P:32, :].bitcast(I32), x_scales[0, e:16:4, :].bitcast(I32))
         xw_table = sb("xw_table", [P, T], U32)
         nc.sync.dma_start(xw_table[:].bitcast(I32), x_words[0].rearrange("p n t -> p (n t)").bitcast(I32))
-        gain = sb("gain", [P, 8], F32)
+        gain_run = sb("gain", [P, 8], F32)
         for r in range(2):
-            nc.sync.dma_start(gain[r:P:2, 0:7], gn.rearrange("(a e) o -> a (e o)", e=8)[:, r : r + 7])
+            nc.sync.dma_start(gain_run[r:P:2, 0:7], gn.rearrange("(a e) o -> a (e o)", e=8)[:, r : r + 7])
+        gain = gain_run[:, 0:7:2]
         load_list("n1", n1)
         load_list("n2", n2)
         w2_raw = sb("w2_raw", [P, PACK, N], F32)
@@ -85,11 +89,12 @@ def tile_picked_layrangeunder_none_p_kernel(
         half_gain = sb("half_gain", [P, PACK], F32)
         half_gain_neg = sb("half_gain_neg", [P, PACK], F32)
         gain_sign = sb("gain_sign", [P, PACK], F32)
-        nc.scalar.activation(half_gain[:], gain[:, 0:7:2], ACT.Abs, scale=0.5)
+        nc.scalar.activation(half_gain[:], gain, ACT.Abs, scale=0.5)
         nc.scalar.activation(half_gain_neg[:], half_gain[:], ACT.Copy, scale=-1.0)
-        nc.scalar.activation(gain_sign[:], gain[:, 0:7:2], ACT.Sign)
+        nc.gpsimd.tensor_scalar(gain_sign[:], gain, 0.0, 2.0, ALU.is_ge, ALU.mult)
+        nc.gpsimd.tensor_scalar(gain_sign[:], gain_sign[:], 1.0, -1.0, ALU.mult, ALU.add)
 
-        def quantize_tile(name, src, t):
+        def quantize_plane(name, src, t):
             codes = sb("%s_codes%d" % (name, t), [P, P], U32)
             scales = sb("%s_scales%d" % (name, t), [P, P], U8)
             nc.vector.quantize_mx(codes[:].bitcast(FP8X4), scales[:], src.rearrange("p m j -> p (m j)"))
@@ -101,36 +106,34 @@ def tile_picked_layrangeunder_none_p_kernel(
                 rhs=codes.bitcast(FP8X4), rhs_scale=scales, start=True, stop=True,
             )
 
-        w1_q = [quantize_tile("w1", w1_bf[:, 0], 0)]
+        w1_q = [quantize_plane("w1", w1_bf[:, 0], 0)]
         xw = []
-        for u in range(2):
-            words = sb("xw%d" % u, [P, HALF], U32)
-            nc.vector.tensor_copy(words[:], xw_table[:].indirect(entries(lists["offs"], u * HALF, (u + 1) * HALF)))
+        for half in range(2):
+            words = sb("xw%d" % half, [P, HALF], U32)
+            nc.vector.tensor_copy(words[:], xw_table[:].indirect(entries("offs", half * HALF, (half + 1) * HALF)))
             xw.append(words)
         for t in range(1, PACK):
-            w1_q.append(quantize_tile("w1", w1_bf[:, t], t))
+            w1_q.append(quantize_plane("w1", w1_bf[:, t], t))
 
-        y_win = [sb("y_win%d" % t, [P, S], F32) for t in range(PACK)]
-        y_half = [sb("y_half%d" % u, [P, PACK, HALF], F32) for u in range(2)]
-        y_own = [y_half[a // HALF][:, :, a % HALF : a % HALF + b - a] for a, b in Z_CHUNKS]
-        y_acc = {}
-
-        def scaled_copy(dst, src, scale, on_vector):
-            if on_vector:
-                nc.vector.tensor_scalar(dst, src, scale, None, ALU.mult)
-            else:
-                nc.scalar.activation(dst, src, ACT.Copy, scale=scale)
-
+        u_win = [sb("y_win%d" % t, [P, S], F32) for t in range(PACK)]
+        u_half = [sb("y_half%d" % half, [P, PACK, HALF], F32) for half in range(2)]
+        u_own = [u_half[a // HALF][:, :, a % HALF : a % HALF + b - a] for a, b in RANGES]
+        second_halves = []
         for t in range(PACK):
-            for u in range(2):
-                acc = bank(2 * t + u, HALF)
-                y_acc[t, u] = acc
-                product(acc[:], w1_q[t], xw[u][:], xs[:, u * HALF : (u + 1) * HALF])
-                scaled_copy(y_win[t][:, u * HALF : (u + 1) * HALF], acc[:], half_gain_neg[:, t : t + 1], (t, u) == (0, 0))
-                if u == 0:
-                    scaled_copy(y_half[0][:, t, :], acc[:], half_gain[:, t : t + 1], t == 0)
+            for half in range(2):
+                acc = bank(2 * t + half, HALF)
+                product(acc[:], w1_q[t], xw[half][:], xs[:, half * HALF : (half + 1) * HALF])
+                window = u_win[t][:, half * HALF : (half + 1) * HALF]
+                if (t, half) == (0, 0):
+                    nc.vector.tensor_scalar(window, acc[:], half_gain[:, 0:1], -1.0, ALU.mult, ALU.mult)
+                    nc.vector.tensor_scalar(u_half[0][:, 0, :], acc[:], half_gain[:, 0:1], None, ALU.mult)
+                else:
+                    nc.scalar.activation(window, acc[:], ACT.Copy, scale=half_gain_neg[:, t : t + 1])
+                    if half == 0:
+                        nc.scalar.activation(u_half[0][:, t, :], acc[:], ACT.Copy, scale=half_gain[:, t : t + 1])
+            second_halves.append(acc)
         for t in range(PACK):
-            nc.scalar.activation(y_half[1][:, t, :], y_acc[t, 1][:], ACT.Copy, scale=half_gain[:, t : t + 1])
+            nc.scalar.activation(u_half[1][:, t, :], second_halves[t][:], ACT.Copy, scale=half_gain[:, t : t + 1])
 
         w2_signed = sb("w2_signed", [P, PACK, N], BF16)
         for j in range(PACK):
@@ -143,41 +146,22 @@ def tile_picked_layrangeunder_none_p_kernel(
                 w2_signed[:].rearrange("p j (a t r) -> p t a j r", t=PACK, r=2)[:, t],
             )
 
-        last = len(Z_CHUNKS) - 1
-        da, db, hi, lo, z_bf = {}, {}, {}, {}, {}
-        z_codes = [sb("z_codes%d" % c, [P, b - a], U32) for c, (a, b) in enumerate(Z_CHUNKS)]
-        z_scales = [sb("z_scales%d" % c, [P, b - a], U8) for c, (a, b) in enumerate(Z_CHUNKS)]
+        d1, d2, most, least, z_bf = {}, {}, {}, {}, {}
+        z_codes = [sb("z_codes%d" % c, [P, b - a], U32) for c, (a, b) in enumerate(RANGES)]
+        z_scales = [sb("z_scales%d" % c, [P, b - a], U8) for c, (a, b) in enumerate(RANGES)]
 
-        def look_up_y(c, t, dst, name):
-            a, b = Z_CHUNKS[c]
-            nc.vector.tensor_tensor(
-                dst[:, t, :], y_win[t][:].indirect(entries(lists[name], a, b)), y_own[c][:, t, :], ALU.add
-            )
+        def look_up_u(c, t, dst, name):
+            a, b = RANGES[c]
+            nc.vector.tensor_tensor(dst[:, t, :], u_win[t][:].indirect(entries(name, a, b)), u_own[c][:, t, :], ALU.add)
 
         def extremes(c):
-            a, b = Z_CHUNKS[c]
-            lo[c] = sb("lo%d" % c, [P, PACK, b - a], F32)
-            hi[c] = sb("hi%d" % c, [P, PACK, b - a], F32)
-            for g in range((b - a) // P):
-                cols = slice(g * P, (g + 1) * P)
-                nc.vector.scalar_tensor_tensor(lo[c][:, :, cols], da[c][:, :, cols], 0.0, db[c][:, :, cols], ALU.min, ALU.min)
-                nc.vector.scalar_tensor_tensor(hi[c][:, :, cols], da[c][:, :, cols], 0.0, db[c][:, :, cols], ALU.max, ALU.max)
-
-        def spread(c, tag):
-            a, b = Z_CHUNKS[c]
-            wide = sb("wide%d" % c, [P, PACK, b - a], F32, tag)
-            nc.vector.scalar_tensor_tensor(wide[:], lo[c][:], -2.0, hi[c][:], ALU.mult, ALU.add)
-            return wide
-
-        def round_z(c, wide):
-            a, b = Z_CHUNKS[c]
-            z_bf[c] = sb("z_bf%d" % c, [P, b - a, PACK], BF16)
-            nc.vector.tensor_tensor(
-                z_bf[c][:].rearrange("p (s i) t -> p s t i", i=2),
-                wide[:].rearrange("p t (s i) -> p s t i", i=2),
-                y_own[c].rearrange("p t (s i) -> p s t i", i=2),
-                ALU.add,
-            )
+            a, b = RANGES[c]
+            least[c] = sb("lo%d" % c, [P, PACK, b - a], F32)
+            most[c] = sb("hi%d" % c, [P, PACK, b - a], F32)
+            for first_col in range(0, b - a, P):
+                cols = slice(first_col, first_col + P)
+                for dst, op in ((least[c], ALU.min), (most[c], ALU.max)):
+                    nc.vector.scalar_tensor_tensor(dst[:, :, cols], d1[c][:, :, cols], 0.0, d2[c][:, :, cols], op, op)
 
         def add_turned(sums, terms):
             steps = [(i, g) for i in range(len(terms)) for g in range(len(terms[0]))]
@@ -188,84 +172,94 @@ def tile_picked_layrangeunder_none_p_kernel(
                 )
 
         def sum_z_on_tensor(c):
-            a, b = Z_CHUNKS[c]
+            a, b = RANGES[c]
             z_bf[c] = sb("z_bf%d" % c, [P, b - a, PACK], BF16)
-            for g in range((b - a) // P):
-                cols = slice(g * P, (g + 1) * P)
-                block = a // P + g
-                lo_twice = sb("lo_twice%d" % block, [P, PACK, P], F32, "chain%d" % min(block, 1))
-                nc.scalar.activation(lo_twice[:], lo[c][:, :, cols], ACT.Copy, scale=-2.0)
+            for first_col in range(0, b - a, P):
+                cols = slice(first_col, first_col + P)
+                block = (a + first_col) // P
+                staging = "chain%d" % min(block, 1)
+                least_twice = sb("lo_twice%d" % block, [P, PACK, P], F32, staging)
+                for pair in range(2):
+                    planes = slice(2 * pair, 2 * pair + 2)
+                    nc.scalar.activation(least_twice[:, planes, :], least[c][:, planes, cols], ACT.Copy, scale=-2.0)
                 sums = bank(2 * (block % 2), PACK * P)
                 add_turned(
                     sums,
                     [
-                        [y_own[c][:, t, cols] for t in range(PACK)],
-                        [hi[c][:, t, cols] for t in range(PACK)],
-                        [lo_twice[:, t, :] for t in range(PACK)],
+                        [u_own[c][:, t, cols] for t in range(PACK)],
+                        [most[c][:, t, cols] for t in range(PACK)],
+                        [least_twice[:, t, :] for t in range(PACK)],
                     ],
                 )
-                pairs = sb("pairs%d" % block, [P, 2, P, 2], BF16, "chain%d" % min(block, 1))
-                nc.scalar.copy(pairs[:], sums[:].rearrange("s (u e p) -> s u p e", u=2, e=2))
+                pairs = sb("pairs%d" % block, [P, 2, P, 2], BF16, staging)
+                nc.scalar.copy(pairs[:], sums[:].rearrange("s (w e p) -> s w p e", w=2, e=2))
                 back = bank(4 + 2 * (block % 2), 2 * P)
-                pair_words = pairs[:].rearrange("s u p e -> s u (p e)").bitcast(F32)
-                for u in range(2):
-                    nc.tensor.transpose(back[:, u * P : (u + 1) * P], pair_words[:, u, :], ident[:])
-                nc.scalar.copy(
-                    z_bf[c][:, cols, :].bitcast(F32), back[:].rearrange("p (u s) -> p s u", u=2)
-                )
+                pair_words = pairs[:].rearrange("s w p e -> s w (p e)").bitcast(F32)
+                for pair in range(2):
+                    nc.tensor.transpose(back[:, pair * P : (pair + 1) * P], pair_words[:, pair, :], ident[:])
+                nc.scalar.copy(z_bf[c][:, cols, :].bitcast(F32), back[:].rearrange("p (w s) -> p s w", w=2))
 
         def quantize_z(c):
             nc.vector.quantize_mx(z_codes[c][:].bitcast(FP8X4), z_scales[c][:], z_bf[c][:].rearrange("p s t -> p (s t)"))
 
-        wide_tiles = range(2, PACK - 1)
-        h_win = [sb("h_win%d" % t, [P, 2 * S if t in wide_tiles else S], F32) for t in range(PACK)]
-        h_own = [
-            h_win[t + 1][:, S:] if t + 1 in wide_tiles else sb("h_own%d" % t, [P, S], F32)[:] for t in range(PACK)
-        ]
+        h_win = [sb("h_win%d" % t, [P, 2 * S if t == WIDE_PLANE else S], F32) for t in range(PACK)]
+        h_own = [h_win[t + 1][:, S:] if t + 1 == WIDE_PLANE else sb("h_own%d" % t, [P, S], F32)[:] for t in range(PACK)]
         w2_q = {}
 
         def second_product(c, t):
-            a, b = Z_CHUNKS[c]
-            acc = bank(2 * t + 1, b - a)
+            a, b = RANGES[c]
+            awaited = (c, t) == (LAST, 0)
+            acc = bank(2 if awaited else 2 * t + 1, b - a)
             product(acc[:], w2_q[t], z_codes[c][:], z_scales[c][:])
-            nc.scalar.activation(h_win[t][:, a:b], acc[:], ACT.Copy, scale=-1.0)
+            if awaited:
+                nc.vector.tensor_scalar(h_win[t][:, a:b], acc[:], -1.0, None, ALU.mult)
+            else:
+                nc.scalar.activation(h_win[t][:, a:b], acc[:], ACT.Copy, scale=-1.0)
             nc.scalar.activation(h_own[t][:, a:b], acc[:], ACT.Copy)
 
-        for c in range(last):
-            a, b = Z_CHUNKS[c]
-            da[c] = sb("da%d" % c, [P, PACK, b - a], F32)
-            db[c] = sb("db%d" % c, [P, PACK, b - a], F32)
+        for c in range(LAST):
+            a, b = RANGES[c]
+            d1[c] = sb("da%d" % c, [P, PACK, b - a], F32)
+            d2[c] = sb("db%d" % c, [P, PACK, b - a], F32)
             for t in range(PACK):
-                look_up_y(c, t, da[c], "n1")
-                look_up_y(c, t, db[c], "n2")
+                look_up_u(c, t, d1[c], "n1")
+                look_up_u(c, t, d2[c], "n2")
             extremes(c)
             sum_z_on_tensor(c)
             deal_w2(2 * c)
             deal_w2(2 * c + 1)
         for t in range(2):
-            w2_q[t] = quantize_tile("w2", w2_bf[t][:], t)
-        da[last] = sb("da%d" % last, [P, PACK, P], F32)
+            w2_q[t] = quantize_plane("w2", w2_bf[t][:], t)
+
+        d1[LAST] = sb("da%d" % LAST, [P, PACK, P], F32)
         for t in range(PACK):
-            look_up_y(last, t, da[last], "n1")
+            look_up_u(LAST, t, d1[LAST], "n1")
         quantize_z(0)
         for t in range(2):
             second_product(0, t)
-        db[last] = sb("db%d" % last, [P, PACK, P], F32, "z_bf0")
+        d2[LAST] = sb("db%d" % LAST, [P, PACK, P], F32, "z_bf0")
         for t in range(PACK):
-            look_up_y(last, t, db[last], "n2")
-        extremes(last)
+            look_up_u(LAST, t, d2[LAST], "n2")
+        extremes(LAST)
+        w2_q[2] = quantize_plane("w2", w2_bf[2][:], 2)
+        spread = sb("wide%d" % LAST, [P, PACK, P], F32)
+        nc.vector.scalar_tensor_tensor(spread[:], least[LAST][:], -2.0, most[LAST][:], ALU.mult, ALU.add)
         quantize_z(1)
         second_product(1, 0)
-        wide = spread(last, "z_bf1")
-        w2_q[2] = quantize_tile("w2", w2_bf[2][:], 2)
-        round_z(last, wide)
-        quantize_z(last)
-        w2_q[3] = quantize_tile("w2", w2_bf[3][:], 3)
-        second_product(last, 0)
+        z_bf[LAST] = sb("z_bf%d" % LAST, [P, P, PACK], BF16, "z_bf1")
+        nc.vector.tensor_tensor(
+            z_bf[LAST][:].rearrange("p (s i) t -> p s t i", i=2),
+            spread[:].rearrange("p t (s i) -> p s t i", i=2),
+            u_own[LAST].rearrange("p t (s i) -> p s t i", i=2),
+            ALU.add,
+        )
+        quantize_z(LAST)
+        w2_q[3] = quantize_plane("w2", w2_bf[3][:], 3)
+        second_product(LAST, 0)
         second_product(1, 1)
-        second_product(last, 1)
+        second_product(LAST, 1)
         for t in range(2, PACK):
-            for c in range(last + 1):
+            for c in range(LAST + 1):
                 second_product(c, t)
 
         out_rows = out.rearrange("(a t r) s -> t a r s", t=PACK, r=2)
@@ -273,56 +267,48 @@ def tile_picked_layrangeunder_none_p_kernel(
         def finish_on_tensor(t):
             first = sb("first%d" % t, [P, S], F32)
             rise = sb("rise%d" % t, [P, S], F32)
-            halves = [slice(u * HALF, (u + 1) * HALF) for u in range(2)]
+            halves = [slice(half * HALF, (half + 1) * HALF) for half in range(2)]
+            blocks = [slice(first_col, first_col + P) for first_col in range(0, HALF, P)]
             for cols in halves:
-                nc.vector.tensor_copy(first[:, cols], h_win[t][:].indirect(entries(lists["n3"], cols.start, cols.stop)))
-            for u, cols in enumerate(halves):
-                nc.vector.tensor_tensor(
-                    rise[:, cols], h_win[t][:].indirect(entries(lists["n4"], cols.start, cols.stop)), first[:, cols], ALU.subtract
-                )
-                lift = sb("lift%d_%d" % (t, u), [P, HALF], F32, "half%d" % u)
+                nc.vector.tensor_copy(first[:, cols], h_win[t][:].indirect(entries("n3", cols.start, cols.stop)))
+            for half, cols in enumerate(halves):
+                looked_up = h_win[t][:].indirect(entries("n4", cols.start, cols.stop))
+                nc.vector.tensor_tensor(rise[:, cols], looked_up, first[:, cols], ALU.subtract)
+                staging = "half%d" % half
+                lift = sb("lift%d_%d" % (t, half), [P, HALF], F32, staging)
                 nc.scalar.activation(lift[:], rise[:, cols], ACT.Relu)
-                sums = bank(2 * u, HALF)
-                blocks = [slice(g * P, (g + 1) * P) for g in range(HALF // P)]
-                add_turned(
-                    sums,
-                    [
-                        [h_own[t][:, cols][:, blk] for blk in blocks],
-                        [first[:, cols][:, blk] for blk in blocks],
-                        [lift[:, blk] for blk in blocks],
-                    ],
-                )
-                turned = sb("turned%d_%d" % (t, u), [P, HALF], F32, "half%d" % u)
+                sums = bank(2 * half, HALF)
+                add_turned(sums, [[term[:, blk] for blk in blocks] for term in (h_own[t][:, cols], first[:, cols], lift)])
+                turned = sb("turned%d_%d" % (t, half), [P, HALF], F32, staging)
                 nc.scalar.copy(turned[:], sums[:])
-                back = bank(4 + 2 * u, HALF)
-                for g in range(HALF // P):
-                    nc.tensor.transpose(back[:, g * P : (g + 1) * P], turned[:, g * P : (g + 1) * P], ident[:])
-                res = sb("res_%d_%d" % (t, u), [P, HALF], F32)
+                back = bank(4 + 2 * half, HALF)
+                for blk in blocks:
+                    nc.tensor.transpose(back[:, blk], turned[:, blk], ident[:])
+                res = sb("res_%d_%d" % (t, half), [P, HALF], F32)
                 nc.scalar.copy(res[:], back[:])
                 nc.sync.dma_start(out_rows[t, :, :, cols], res[:])
 
-        for t in range(2):
+        for t in range(TURNED_PLANES):
             finish_on_tensor(t)
 
-        pieces = [(t, 0, S) for t in wide_tiles]
-        pieces = pieces + [(PACK - 1, a, b) for a, b in Z_CHUNKS]
         gaps = {}
 
         def look_up_h(piece):
             t, a, b = piece
             for name in ("n3", "n4"):
                 gap = sb("gap_%s_%d_%d" % (name, t, a), [P, b - a], F32)
-                nc.vector.tensor_tensor(gap[:], h_win[t][:].indirect(entries(lists[name], a, b)), h_own[t][:, a:b], ALU.add)
+                nc.vector.tensor_tensor(gap[:], h_win[t][:].indirect(entries(name, a, b)), h_own[t][:, a:b], ALU.add)
                 gaps[name, piece] = gap
 
-        def finish(piece):
+        def finish_on_vector(piece):
             t, a, b = piece
             res = sb("res_last_%d_%d" % (t, a), [P, b - a], F32)
             nc.vector.tensor_tensor(res[:], gaps["n3", piece][:], gaps["n4", piece][:], ALU.max)
             nc.sync.dma_start(out_rows[t, :, :, a:b], res[:])
 
+        pieces = [(WIDE_PLANE, 0, S)] + [(PACK - 1, a, b) for a, b in RANGES]
         look_up_h(pieces[0])
         for before, piece in zip(pieces, pieces[1:]):
             look_up_h(piece)
-            finish(before)
-        finish(pieces[-1])
+            finish_on_vector(before)
+        finish_on_vector(pieces[-1])

from contextlib import ExitStack

import concourse.mybir as mybir
from concourse.masks import make_identity

K, T, S, H, N = 512, 2048, 512, 512, 512
FLOPS = 2 * K * H * S + 2 * H * N * S

F32 = mybir.dt.float32
BF16 = mybir.dt.bfloat16
I32 = mybir.dt.int32
U32 = mybir.dt.uint32
U16 = mybir.dt.uint16
U8 = mybir.dt.uint8
FP8X4 = mybir.dt.float8_e4m3fn_x4
ALU = mybir.AluOpType
ACT = mybir.ActivationFunctionType

P = 128
PACK = 4
STRIPE = 16
HALF = S // 2
RANGES = [(0, 256), (256, 384), (384, 512)]
LAST = len(RANGES) - 1
TURNED_PLANES = 2
WIDE_PLANE = 2


def tile_picked_layrangeunder_none_p_kernel(
    tc, x_words, x_scales, w1, gn, w2, offs, n1, n2, n3, n4, out
):
    nc = tc.nc
    with ExitStack() as ctx:
        pool = ctx.enter_context(tc.tile_pool(name="sbuf", bufs=1))
        psum = ctx.enter_context(tc.psum_pool(name="psum", bufs=1))

        def sb(name, shape, dtype, tag=None):
            return pool.tile(shape, dtype, name=name, tag=tag or name, align_bytes=64)

        def bank(number, width):
            return psum.tile([P, width], F32, name="bank%d" % number)

        lists = {}

        def load_list(name, src):
            lists[name] = sb("list_" + name, [P, S // STRIPE], U16)
            nc.sync.dma_start(lists[name][:], src)

        def entries(name, a, b):
            return lists[name][:, a // STRIPE : b // STRIPE]

        xs_table = sb("xs_table", [P, T], U8)
        nc.gpsimd.memset(xs_table[:].bitcast(I32), 0)
        load_list("offs", offs)
        w1_rows = w1.rearrange("(p j) c -> p j c", j=PACK)
        w1_raw = []
        for pair in range(2):
            raw = sb("w1_raw%d" % pair, [P, 2, H], F32)
            nc.sync.dma_start(raw[:], w1_rows[:, 2 * pair : 2 * pair + 2, :])
            w1_raw.append(raw)
            if pair == 0:
                for e in range(4):
                    nc.sync.dma_start(xs_table[e:P:32, :].bitcast(I32), x_scales[0, e:16:4, :].bitcast(I32))
        xw_table = sb("xw_table", [P, T], U32)
        nc.sync.dma_start(xw_table[:].bitcast(I32), x_words[0].rearrange("p n t -> p (n t)").bitcast(I32))
        gain_run = sb("gain", [P, 8], F32)
        for r in range(2):
            nc.sync.dma_start(gain_run[r:P:2, 0:7], gn.rearrange("(a e) o -> a (e o)", e=8)[:, r : r + 7])
        gain = gain_run[:, 0:7:2]
        load_list("n1", n1)
        load_list("n2", n2)
        w2_raw = sb("w2_raw", [P, PACK, N], F32)
        for r in range(2):
            nc.sync.dma_start(w2_raw[r:P:2], w2.rearrange("(a j r) c -> r a j c", j=PACK, r=2)[r])
        load_list("n3", n3)
        load_list("n4", n4)

        ident = sb("ident", [P, P], F32)
        make_identity(nc, ident[:])

        xs = sb("xs", [P, S], U8)
        nc.vector.tensor_copy(xs[:], xs_table[:].indirect(lists["offs"][:]))

        w1_bf = sb("w1_bf", [P, PACK, P, PACK], BF16)
        dealt = w1_bf[:].rearrange("p t (a r) j -> p a t j r", r=2)
        nc.scalar.copy(dealt[:, :, :, 0:2], w1_raw[0][:].rearrange("p j (a t r) -> p a t j r", t=PACK, r=2))
        nc.vector.tensor_copy(dealt[:, :, :, 2:4], w1_raw[1][:].rearrange("p j (a t r) -> p a t j r", t=PACK, r=2))

        half_gain = sb("half_gain", [P, PACK], F32)
        half_gain_neg = sb("half_gain_neg", [P, PACK], F32)
        gain_sign = sb("gain_sign", [P, PACK], F32)
        nc.scalar.activation(half_gain[:], gain, ACT.Abs, scale=0.5)
        nc.scalar.activation(half_gain_neg[:], half_gain[:], ACT.Copy, scale=-1.0)
        nc.gpsimd.tensor_scalar(gain_sign[:], gain, 0.0, 2.0, ALU.is_ge, ALU.mult)
        nc.gpsimd.tensor_scalar(gain_sign[:], gain_sign[:], 1.0, -1.0, ALU.mult, ALU.add)

        def quantize_plane(name, src, t):
            codes = sb("%s_codes%d" % (name, t), [P, P], U32)
            scales = sb("%s_scales%d" % (name, t), [P, P], U8)
            nc.vector.quantize_mx(codes[:].bitcast(FP8X4), scales[:], src.rearrange("p m j -> p (m j)"))
            return codes, scales

        def product(acc, weights, codes, scales):
            nc.tensor.matmul_mx(
                acc, lhsT=weights[0][:].bitcast(FP8X4), lhsT_scale=weights[1][:],
                rhs=codes.bitcast(FP8X4), rhs_scale=scales, start=True, stop=True,
            )

        w1_q = [quantize_plane("w1", w1_bf[:, 0], 0)]
        xw = []
        for half in range(2):
            words = sb("xw%d" % half, [P, HALF], U32)
            nc.vector.tensor_copy(words[:], xw_table[:].indirect(entries("offs", half * HALF, (half + 1) * HALF)))
            xw.append(words)
        for t in range(1, PACK):
            w1_q.append(quantize_plane("w1", w1_bf[:, t], t))

        u_win = [sb("y_win%d" % t, [P, S], F32) for t in range(PACK)]
        u_half = [sb("y_half%d" % half, [P, PACK, HALF], F32) for half in range(2)]
        u_own = [u_half[a // HALF][:, :, a % HALF : a % HALF + b - a] for a, b in RANGES]
        second_halves = []
        for t in range(PACK):
            for half in range(2):
                acc = bank(2 * t + half, HALF)
                product(acc[:], w1_q[t], xw[half][:], xs[:, half * HALF : (half + 1) * HALF])
                window = u_win[t][:, half * HALF : (half + 1) * HALF]
                if (t, half) == (0, 0):
                    nc.vector.tensor_scalar(window, acc[:], half_gain[:, 0:1], -1.0, ALU.mult, ALU.mult)
                    nc.vector.tensor_scalar(u_half[0][:, 0, :], acc[:], half_gain[:, 0:1], None, ALU.mult)
                else:
                    nc.scalar.activation(window, acc[:], ACT.Copy, scale=half_gain_neg[:, t : t + 1])
                    if half == 0:
                        nc.scalar.activation(u_half[0][:, t, :], acc[:], ACT.Copy, scale=half_gain[:, t : t + 1])
            second_halves.append(acc)
        for t in range(PACK):
            nc.scalar.activation(u_half[1][:, t, :], second_halves[t][:], ACT.Copy, scale=half_gain[:, t : t + 1])

        w2_signed = sb("w2_signed", [P, PACK, N], BF16)
        for j in range(PACK):
            nc.scalar.activation(w2_signed[:, j, :], w2_raw[:, j, :], ACT.Copy, scale=gain_sign[:, j : j + 1])
        w2_bf = [sb("w2_bf%d" % t, [P, P, PACK], BF16) for t in range(PACK)]

        def deal_w2(t):
            nc.scalar.copy(
                w2_bf[t][:].rearrange("p (a r) j -> p a j r", r=2),
                w2_signed[:].rearrange("p j (a t r) -> p t a j r", t=PACK, r=2)[:, t],
            )

        d1, d2, most, least, z_bf = {}, {}, {}, {}, {}
        z_codes = [sb("z_codes%d" % c, [P, b - a], U32) for c, (a, b) in enumerate(RANGES)]
        z_scales = [sb("z_scales%d" % c, [P, b - a], U8) for c, (a, b) in enumerate(RANGES)]

        def look_up_u(c, t, dst, name):
            a, b = RANGES[c]
            nc.vector.tensor_tensor(dst[:, t, :], u_win[t][:].indirect(entries(name, a, b)), u_own[c][:, t, :], ALU.add)

        def extremes(c):
            a, b = RANGES[c]
            least[c] = sb("lo%d" % c, [P, PACK, b - a], F32)
            most[c] = sb("hi%d" % c, [P, PACK, b - a], F32)
            for first_col in range(0, b - a, P):
                cols = slice(first_col, first_col + P)
                for dst, op in ((least[c], ALU.min), (most[c], ALU.max)):
                    nc.vector.scalar_tensor_tensor(dst[:, :, cols], d1[c][:, :, cols], 0.0, d2[c][:, :, cols], op, op)

        def add_turned(sums, terms):
            steps = [(i, g) for i in range(len(terms)) for g in range(len(terms[0]))]
            for i, g in steps:
                nc.tensor.matmul(
                    sums[:, g * P : (g + 1) * P], terms[i][g], ident[:],
                    start=(i, g) == steps[0], stop=(i, g) == steps[-1], is_transpose=True,
                )

        def sum_z_on_tensor(c):
            a, b = RANGES[c]
            z_bf[c] = sb("z_bf%d" % c, [P, b - a, PACK], BF16)
            for first_col in range(0, b - a, P):
                cols = slice(first_col, first_col + P)
                block = (a + first_col) // P
                staging = "chain%d" % min(block, 1)
                least_twice = sb("lo_twice%d" % block, [P, PACK, P], F32, staging)
                for pair in range(2):
                    planes = slice(2 * pair, 2 * pair + 2)
                    nc.scalar.activation(least_twice[:, planes, :], least[c][:, planes, cols], ACT.Copy, scale=-2.0)
                sums = bank(2 * (block % 2), PACK * P)
                add_turned(
                    sums,
                    [
                        [u_own[c][:, t, cols] for t in range(PACK)],
                        [most[c][:, t, cols] for t in range(PACK)],
                        [least_twice[:, t, :] for t in range(PACK)],
                    ],
                )
                pairs = sb("pairs%d" % block, [P, 2, P, 2], BF16, staging)
                nc.scalar.copy(pairs[:], sums[:].rearrange("s (w e p) -> s w p e", w=2, e=2))
                back = bank(4 + 2 * (block % 2), 2 * P)
                pair_words = pairs[:].rearrange("s w p e -> s w (p e)").bitcast(F32)
                for pair in range(2):
                    nc.tensor.transpose(back[:, pair * P : (pair + 1) * P], pair_words[:, pair, :], ident[:])
                nc.scalar.copy(z_bf[c][:, cols, :].bitcast(F32), back[:].rearrange("p (w s) -> p s w", w=2))

        def quantize_z(c):
            nc.vector.quantize_mx(z_codes[c][:].bitcast(FP8X4), z_scales[c][:], z_bf[c][:].rearrange("p s t -> p (s t)"))

        h_win = [sb("h_win%d" % t, [P, 2 * S if t == WIDE_PLANE else S], F32) for t in range(PACK)]
        h_own = [h_win[t + 1][:, S:] if t + 1 == WIDE_PLANE else sb("h_own%d" % t, [P, S], F32)[:] for t in range(PACK)]
        w2_q = {}

        def second_product(c, t):
            a, b = RANGES[c]
            awaited = (c, t) == (LAST, 0)
            acc = bank(2 if awaited else 2 * t + 1, b - a)
            product(acc[:], w2_q[t], z_codes[c][:], z_scales[c][:])
            if awaited:
                nc.vector.tensor_scalar(h_win[t][:, a:b], acc[:], -1.0, None, ALU.mult)
            else:
                nc.scalar.activation(h_win[t][:, a:b], acc[:], ACT.Copy, scale=-1.0)
            nc.scalar.activation(h_own[t][:, a:b], acc[:], ACT.Copy)

        for c in range(LAST):
            a, b = RANGES[c]
            d1[c] = sb("da%d" % c, [P, PACK, b - a], F32)
            d2[c] = sb("db%d" % c, [P, PACK, b - a], F32)
            for t in range(PACK):
                look_up_u(c, t, d1[c], "n1")
                look_up_u(c, t, d2[c], "n2")
            extremes(c)
            sum_z_on_tensor(c)
            deal_w2(2 * c)
            deal_w2(2 * c + 1)
        for t in range(2):
            w2_q[t] = quantize_plane("w2", w2_bf[t][:], t)

        d1[LAST] = sb("da%d" % LAST, [P, PACK, P], F32)
        for t in range(PACK):
            look_up_u(LAST, t, d1[LAST], "n1")
        quantize_z(0)
        for t in range(2):
            second_product(0, t)
        d2[LAST] = sb("db%d" % LAST, [P, PACK, P], F32, "z_bf0")
        for t in range(PACK):
            look_up_u(LAST, t, d2[LAST], "n2")
        extremes(LAST)
        w2_q[2] = quantize_plane("w2", w2_bf[2][:], 2)
        spread = sb("wide%d" % LAST, [P, PACK, P], F32)
        nc.vector.scalar_tensor_tensor(spread[:], least[LAST][:], -2.0, most[LAST][:], ALU.mult, ALU.add)
        quantize_z(1)
        second_product(1, 0)
        z_bf[LAST] = sb("z_bf%d" % LAST, [P, P, PACK], BF16, "z_bf1")
        nc.vector.tensor_tensor(
            z_bf[LAST][:].rearrange("p (s i) t -> p s t i", i=2),
            spread[:].rearrange("p t (s i) -> p s t i", i=2),
            u_own[LAST].rearrange("p t (s i) -> p s t i", i=2),
            ALU.add,
        )
        quantize_z(LAST)
        w2_q[3] = quantize_plane("w2", w2_bf[3][:], 3)
        second_product(LAST, 0)
        second_product(1, 1)
        second_product(LAST, 1)
        for t in range(2, PACK):
            for c in range(LAST + 1):
                second_product(c, t)

        out_rows = out.rearrange("(a t r) s -> t a r s", t=PACK, r=2)

        def finish_on_tensor(t):
            first = sb("first%d" % t, [P, S], F32)
            rise = sb("rise%d" % t, [P, S], F32)
            halves = [slice(half * HALF, (half + 1) * HALF) for half in range(2)]
            blocks = [slice(first_col, first_col + P) for first_col in range(0, HALF, P)]
            for cols in halves:
                nc.vector.tensor_copy(first[:, cols], h_win[t][:].indirect(entries("n3", cols.start, cols.stop)))
            for half, cols in enumerate(halves):
                looked_up = h_win[t][:].indirect(entries("n4", cols.start, cols.stop))
                nc.vector.tensor_tensor(rise[:, cols], looked_up, first[:, cols], ALU.subtract)
                staging = "half%d" % half
                lift = sb("lift%d_%d" % (t, half), [P, HALF], F32, staging)
                nc.scalar.activation(lift[:], rise[:, cols], ACT.Relu)
                sums = bank(2 * half, HALF)
                add_turned(sums, [[term[:, blk] for blk in blocks] for term in (h_own[t][:, cols], first[:, cols], lift)])
                turned = sb("turned%d_%d" % (t, half), [P, HALF], F32, staging)
                nc.scalar.copy(turned[:], sums[:])
                back = bank(4 + 2 * half, HALF)
                for blk in blocks:
                    nc.tensor.transpose(back[:, blk], turned[:, blk], ident[:])
                res = sb("res_%d_%d" % (t, half), [P, HALF], F32)
                nc.scalar.copy(res[:], back[:])
                nc.sync.dma_start(out_rows[t, :, :, cols], res[:])

        for t in range(TURNED_PLANES):
            finish_on_tensor(t)

        gaps = {}

        def look_up_h(piece):
            t, a, b = piece
            for name in ("n3", "n4"):
                gap = sb("gap_%s_%d_%d" % (name, t, a), [P, b - a], F32)
                nc.vector.tensor_tensor(gap[:], h_win[t][:].indirect(entries(name, a, b)), h_own[t][:, a:b], ALU.add)
                gaps[name, piece] = gap

        def finish_on_vector(piece):
            t, a, b = piece
            res = sb("res_last_%d_%d" % (t, a), [P, b - a], F32)
            nc.vector.tensor_tensor(res[:], gaps["n3", piece][:], gaps["n4", piece][:], ALU.max)
            nc.sync.dma_start(out_rows[t, :, :, a:b], res[:])

        pieces = [(WIDE_PLANE, 0, S)] + [(PACK - 1, a, b) for a, b in RANGES]
        look_up_h(pieces[0])
        for before, piece in zip(pieces, pieces[1:]):
            look_up_h(piece)
            finish_on_vector(before)
        finish_on_vector(pieces[-1])
